import numpy as np
import ml_dtypes


def mxq(x, axis, fmt="e4m3"):
    dtype, down = {"e4m3": (ml_dtypes.float8_e4m3fn, 7), "e5m2": (ml_dtypes.float8_e5m2, 14)}[fmt]
    v = np.moveaxis(np.asarray(x, np.float32).astype(ml_dtypes.bfloat16).astype(np.float64), axis, -1)
    blocks = v.reshape(v.shape[:-1] + (-1, 32))
    amax = np.abs(blocks).max(-1, keepdims=True)
    byte = np.maximum(np.where(amax > 0, np.frexp(amax)[1] - 1 + 127, 0) - down, 1)
    scale = np.exp2(byte - 127.0)
    codes = (blocks / scale).astype(np.float32).astype(dtype).astype(np.float64)
    return np.moveaxis((codes * scale).reshape(v.shape), -1, axis)


WIDE = False


def mx_kscale(k):
    if not WIDE:
        return np.ones(k)
    levels = np.array([10, -10, 5, -5, 0])
    if k % 512:
        return np.exp2(np.random.permutation(np.resize(levels, k // 32))).repeat(32)
    a = np.empty((k // 512, 16))
    for p in range(k // 512):
        a[p, :8] = np.random.permutation(np.resize(levels, 8))
        for g in range(8):
            far = levels[np.abs(levels - a[p, g]) >= 10]
            a[p, g + 8] = far[np.random.randint(len(far))]
    return np.exp2(a.ravel()).repeat(32)


def f64(x):
    return np.asarray(x).astype(np.float64)


def striped(idx):
    return np.tile(idx.reshape(-1, 16).T, (8, 1)).astype(np.uint16)


def unstriped(offs):
    return offs[:16].T.reshape(-1).astype(np.int64)


def pack_weight(w):
    k, n = w.shape
    w = f64(np.asarray(w, np.float32).astype(ml_dtypes.bfloat16)).reshape(k // 32, 32, n)
    amax = np.abs(w).max(1)
    byte = np.clip(np.where(amax > 0, np.frexp(amax)[1] - 1 + 127 - 7, 1), 1, 254)
    scaled = (w * np.exp2(127.0 - byte)[:, None, :]).reshape(k, n).astype(np.float32)
    words = np.ascontiguousarray(scaled.reshape(k // 512, 128, 4, n).transpose(0, 1, 3, 2)).astype(ml_dtypes.float8_e4m3fn).view(np.uint8)
    return words, np.ascontiguousarray(byte.astype(np.uint8).reshape(k // 512, 16, n))


def unpack_weight(words, scales):
    g, p, n, _ = words.shape
    vals = np.ascontiguousarray(words).view(ml_dtypes.float8_e4m3fn).astype(np.float64) * np.repeat(np.exp2(scales.astype(np.float64) - 127.0), 8, axis=1)[..., None]
    return vals.transpose(0, 1, 3, 2).reshape(g * 512, n)


def sigmoid(v):
    return 1.0 / (1.0 + np.exp(-np.maximum(v, -700.0)))


K, T, S, H, N = 512, 1024, 512, 512, 128


def setup_inputs():
    n = np.random.standard_normal
    s = mx_kscale(K)[:, None]
    u = mx_kscale(H)
    packed = pack_weight(n((K, T)) * s)
    return {
        "x_words": packed[0],
        "x_scales": packed[1],
        "w1": (n((K, H)) / np.sqrt(K) / s).astype(np.float32),
        "w3": (n((K, H)) / np.sqrt(K) / s * u).astype(np.float32),
        "w2": (n((H, N)) / np.sqrt(H) / u[:, None]).astype(np.float32),
        "offs": striped(np.sort(np.random.permutation(T)[:S])),
    }


def reference(x_words, x_scales, w1, w3, w2, offs):
    idx = unstriped(offs)
    xq = unpack_weight(x_words, x_scales)[:, idx]
    h = sigmoid(mxq(f64(w1), 0, "e4m3").T @ xq) * (mxq(f64(w3), 0, "e4m3").T @ xq)
    y = mxq(f64(w2), 0, "e4m3").T @ mxq(h, 0, "e4m3")
    return y

@@ -1,0 +1,160 @@
+from contextlib import ExitStack
+
+import concourse.mybir as mybir
+
+K, T, S, H, N = 512, 1024, 512, 512, 128
+FLOPS = 2 * S * (2 * K * H + H * N)
+
+F32 = mybir.dt.float32
+BF16 = mybir.dt.bfloat16
+I32 = mybir.dt.int32
+U32 = mybir.dt.uint32
+U16 = mybir.dt.uint16
+U8 = mybir.dt.uint8
+FP8X4 = mybir.dt.float8_e4m3fn_x4
+SIGMOID = mybir.ActivationFunctionType.Sigmoid
+MULT = mybir.AluOpType.mult
+
+P = 128
+PACK = 4
+TOK = 128
+BLOCKS = S // TOK
+HALF = H // 2
+HM = HALF // PACK
+
+
+def tile_picked_pick_glu_sigmoid_srt_p_kernel(tc, x_words, x_scales, w1, w3, w2, offs, out):
+    nc = tc.nc
+    with ExitStack() as ctx:
+        keep = ctx.enter_context(tc.tile_pool(name="keep", bufs=1))
+        psum = ctx.enter_context(tc.psum_pool(name="psum", bufs=BLOCKS))
+
+        offsets = keep.tile([P, S // 16], U16, name="offsets")
+        nc.sync.dma_start(offsets[:], offs)
+
+        all_scales = keep.tile([P, T], U8, name="all_scales", align_bytes=64)
+        nc.vector.memset(all_scales[:].bitcast(I32), 0)
+        for q in range(4):
+            nc.scalar.dma_start(
+                all_scales[32 * q : 32 * q + 4, :].bitcast(I32),
+                x_scales[0, 4 * q : 4 * q + 4, :].bitcast(I32),
+            )
+        warm_in = keep.tile([P, 1], F32, name="warm_in")
+        warm_out = keep.tile([P, 1], F32, name="warm_out")
+        nc.vector.memset(warm_in[:], 0.0)
+        nc.scalar.activation(warm_out[:], warm_in[:], SIGMOID)
+
+        def load_half(w, half, name):
+            raw = keep.tile([P, PACK, HALF], F32, name=name)
+            nc.sync.dma_start(raw[:], w.rearrange("(p j) c -> p j c", j=PACK)[:, :, half * HALF : (half + 1) * HALF])
+            return raw
+
+        w1_raw = [load_half(w1, half, "w1_raw%d" % half) for half in range(2)]
+        all_words = keep.tile([P, T], I32, name="all_words", align_bytes=64)
+        nc.sync.dma_start(all_words[:], x_words[0].rearrange("p c r -> p (c r)").bitcast(I32))
+        w3_raw = [load_half(w3, half, "w3_raw%d" % half) for half in range(2)]
+        w2_raw = keep.tile([P, PACK, N], F32, name="w2_raw")
+        nc.sync.dma_start(w2_raw[:], w2.rearrange("(p j) n -> p j n", j=PACK))
+
+        x_sc = keep.tile([P, S], U8, name="x_sc", align_bytes=64)
+        nc.vector.tensor_copy(x_sc[:], all_scales[:].indirect(offsets[:]))
+
+        def deal(copy, grouped, raw, t0, t1):
+            copy(
+                grouped[:, t0:t1, :, :].rearrange("p t m j -> p m t j"),
+                raw[:].rearrange("p j (m t) -> p m t j", t=PACK)[:, :, t0:t1, :],
+            )
+
+        def quantise_half(codes, scales, grouped, half):
+            cols = slice(half * HM, (half + 1) * HM)
+            for t in range(PACK):
+                nc.vector.quantize_mx(
+                    out=codes[t][:, cols].bitcast(FP8X4),
+                    scales=scales[t][:, cols],
+                    in_=grouped[:, t, :, :].rearrange("p m j -> p (m j)"),
+                )
+
+        def weight_tiles(name):
+            grouped = [keep.tile([P, PACK, HM, PACK], BF16, name="%s_g%d" % (name, h), align_bytes=64) for h in range(2)]
+            codes = [keep.tile([P, P], U32, name="%s_c%d" % (name, t), align_bytes=64) for t in range(PACK)]
+            scales = [keep.tile([P, P], U8, name="%s_s%d" % (name, t), align_bytes=64) for t in range(PACK)]
+            return grouped, codes, scales
+
+        w1_g, w1_c, w1_s = weight_tiles("w1")
+        w3_g, w3_c, w3_s = weight_tiles("w3")
+
+        deal(nc.scalar.copy, w1_g[0], w1_raw[0], 0, 4)
+        deal(nc.vector.tensor_copy, w1_g[1], w1_raw[1], 0, 2)
+        deal(nc.scalar.copy, w1_g[1], w1_raw[1], 2, 4)
+        quantise_half(w1_c, w1_s, w1_g[0], 0)
+        quantise_half(w1_c, w1_s, w1_g[1], 1)
+
+        x_w = []
+        for b in range(BLOCKS):
+            words = keep.tile([P, TOK], U32, name="x_w%d" % b, align_bytes=64)
+            nc.vector.tensor_copy(
+                words[:], all_words[:].bitcast(U32).indirect(offsets[:, b * (TOK // 16) : (b + 1) * (TOK // 16)])
+            )
+            x_w.append(words)
+
+        def first_layer(codes, scales, b, tag):
+            bank = psum.tile([P, PACK, TOK], F32, name="%s%d" % (tag, b), tag=tag)
+            for t in range(PACK):
+                nc.tensor.matmul_mx(
+                    out=bank[:, t, :],
+                    lhsT=codes[t][:].bitcast(FP8X4),
+                    lhsT_scale=scales[t][:],
+                    rhs=x_w[b][:].bitcast(FP8X4),
+                    rhs_scale=x_sc[:, b * TOK : (b + 1) * TOK],
+                    start=True,
+                    stop=True,
+                )
+            return bank
+
+        gates = []
+        for b in range(BLOCKS):
+            bank = first_layer(w1_c, w1_s, b, "gate")
+            gate = keep.tile([P, TOK, PACK], F32, name="sig%d" % b)
+            nc.scalar.activation(gate[:], bank[:].rearrange("p t n -> p n t"), SIGMOID)
+            gates.append(gate)
+
+        deal(nc.vector.tensor_copy, w3_g[0], w3_raw[0], 0, 4)
+        quantise_half(w3_c, w3_s, w3_g[0], 0)
+        deal(nc.vector.tensor_copy, w3_g[1], w3_raw[1], 0, 4)
+        quantise_half(w3_c, w3_s, w3_g[1], 1)
+
+        w2_g = keep.tile([P, N, PACK], BF16, name="w2_g", align_bytes=64)
+        w2_c = keep.tile([P, N], U32, name="w2_c", align_bytes=64)
+        w2_s = keep.tile([P, N], U8, name="w2_s", align_bytes=64)
+        nc.scalar.copy(w2_g[:], w2_raw[:].rearrange("p j n -> p n j"))
+
+        def hidden(b):
+            bank = first_layer(w3_c, w3_s, b, "up")
+            h = keep.tile([P, TOK, PACK], BF16, name="h%d" % b, align_bytes=64)
+            nc.vector.tensor_tensor(h[:], bank[:].rearrange("p t n -> p n t"), gates[b][:], MULT)
+            return h
+
+        def second_layer(h, b):
+            h_c = keep.tile([P, TOK], U32, name="h_c%d" % b, align_bytes=64)
+            h_s = keep.tile([P, TOK], U8, name="h_s%d" % b, align_bytes=64)
+            nc.vector.quantize_mx(out=h_c[:].bitcast(FP8X4), scales=h_s[:], in_=h[:].rearrange("p n t -> p (n t)"))
+            bank = psum.tile([P, TOK], F32, name="y%d" % b, tag="gate")
+            nc.tensor.matmul_mx(
+                out=bank[:],
+                lhsT=w2_c[:].bitcast(FP8X4),
+                lhsT_scale=w2_s[:],
+                rhs=h_c[:].bitcast(FP8X4),
+                rhs_scale=h_s[:],
+                start=True,
+                stop=True,
+            )
+            y = keep.tile([P, TOK], F32, name="y_sb%d" % b)
+            nc.scalar.copy(y[:], bank[:])
+            nc.sync.dma_start(out[:, b * TOK : (b + 1) * TOK], y[:])
+
+        hs = [hidden(0), hidden(1)]
+        nc.vector.quantize_mx(out=w2_c[:].bitcast(FP8X4), scales=w2_s[:], in_=w2_g[:].rearrange("p n j -> p (n j)"))
+        for b in range(BLOCKS):
+            second_layer(hs[b], b)
+            if b + 2 < BLOCKS:
+                hs.append(hidden(b + 2))

@@ -21,73 +21,37 @@ TOK = 128
 BLOCKS = S // TOK
 HALF = H // 2
 HM = HALF // PACK
+SLOT_ORDER = (2, 3, 0, 1)
 
 
 def tile_picked_pick_glu_sigmoid_srt_p_kernel(tc, x_words, x_scales, w1, w3, w2, offs, out):
     nc = tc.nc
     with ExitStack() as ctx:
         keep = ctx.enter_context(tc.tile_pool(name="keep", bufs=1))
-        psum = ctx.enter_context(tc.psum_pool(name="psum", bufs=BLOCKS))
-
-        offsets = keep.tile([P, S // 16], U16, name="offsets")
-        nc.sync.dma_start(offsets[:], offs)
+        psum = ctx.enter_context(tc.psum_pool(name="psum", bufs=1))
 
         all_scales = keep.tile([P, T], U8, name="all_scales", align_bytes=64)
         nc.vector.memset(all_scales[:].bitcast(I32), 0)
-        for q in range(4):
-            nc.scalar.dma_start(
-                all_scales[32 * q : 32 * q + 4, :].bitcast(I32),
-                x_scales[0, 4 * q : 4 * q + 4, :].bitcast(I32),
-            )
         warm_in = keep.tile([P, 1], F32, name="warm_in")
         warm_out = keep.tile([P, 1], F32, name="warm_out")
         nc.vector.memset(warm_in[:], 0.0)
         nc.scalar.activation(warm_out[:], warm_in[:], SIGMOID)
 
         def load_half(w, half, name):
-            raw = keep.tile([P, PACK, HALF], F32, name=name)
+            raw = keep.tile([P, PACK, HALF], F32, name=name, tag=name)
             nc.sync.dma_start(raw[:], w.rearrange("(p j) c -> p j c", j=PACK)[:, :, half * HALF : (half + 1) * HALF])
             return raw
 
-        w1_raw = [load_half(w1, half, "w1_raw%d" % half) for half in range(2)]
         all_words = keep.tile([P, T], I32, name="all_words", align_bytes=64)
         nc.sync.dma_start(all_words[:], x_words[0].rearrange("p c r -> p (c r)").bitcast(I32))
+        offsets = keep.tile([P, S // 16], U16, name="offsets")
+        nc.sync.dma_start(offsets[:], offs)
+        for r in range(4):
+            nc.sync.dma_start(all_scales[r:P:32, :].bitcast(I32), x_scales[0, r:16:4, :].bitcast(I32))
+        w1_raw = [load_half(w1, half, "w1_raw%d" % half) for half in range(2)]
         w3_raw = [load_half(w3, half, "w3_raw%d" % half) for half in range(2)]
         w2_raw = keep.tile([P, PACK, N], F32, name="w2_raw")
         nc.sync.dma_start(w2_raw[:], w2.rearrange("(p j) n -> p j n", j=PACK))
-
-        x_sc = keep.tile([P, S], U8, name="x_sc", align_bytes=64)
-        nc.vector.tensor_copy(x_sc[:], all_scales[:].indirect(offsets[:]))
-
-        def deal(copy, grouped, raw, t0, t1):
-            copy(
-                grouped[:, t0:t1, :, :].rearrange("p t m j -> p m t j"),
-                raw[:].rearrange("p j (m t) -> p m t j", t=PACK)[:, :, t0:t1, :],
-            )
-
-        def quantise_half(codes, scales, grouped, half):
-            cols = slice(half * HM, (half + 1) * HM)
-            for t in range(PACK):
-                nc.vector.quantize_mx(
-                    out=codes[t][:, cols].bitcast(FP8X4),
-                    scales=scales[t][:, cols],
-                    in_=grouped[:, t, :, :].rearrange("p m j -> p (m j)"),
-                )
-
-        def weight_tiles(name):
-            grouped = [keep.tile([P, PACK, HM, PACK], BF16, name="%s_g%d" % (name, h), align_bytes=64) for h in range(2)]
-            codes = [keep.tile([P, P], U32, name="%s_c%d" % (name, t), align_bytes=64) for t in range(PACK)]
-            scales = [keep.tile([P, P], U8, name="%s_s%d" % (name, t), align_bytes=64) for t in range(PACK)]
-            return grouped, codes, scales
-
-        w1_g, w1_c, w1_s = weight_tiles("w1")
-        w3_g, w3_c, w3_s = weight_tiles("w3")
-
-        deal(nc.scalar.copy, w1_g[0], w1_raw[0], 0, 4)
-        deal(nc.vector.tensor_copy, w1_g[1], w1_raw[1], 0, 2)
-        deal(nc.scalar.copy, w1_g[1], w1_raw[1], 2, 4)
-        quantise_half(w1_c, w1_s, w1_g[0], 0)
-        quantise_half(w1_c, w1_s, w1_g[1], 1)
 
         x_w = []
         for b in range(BLOCKS):
@@ -97,64 +61,108 @@ def tile_picked_pick_glu_sigmoid_srt_p_kernel(tc, x_words, x_scales, w1, w3, w2,
             )
             x_w.append(words)
 
-        def first_layer(codes, scales, b, tag):
-            bank = psum.tile([P, PACK, TOK], F32, name="%s%d" % (tag, b), tag=tag)
-            for t in range(PACK):
-                nc.tensor.matmul_mx(
-                    out=bank[:, t, :],
-                    lhsT=codes[t][:].bitcast(FP8X4),
-                    lhsT_scale=scales[t][:],
-                    rhs=x_w[b][:].bitcast(FP8X4),
-                    rhs_scale=x_sc[:, b * TOK : (b + 1) * TOK],
-                    start=True,
-                    stop=True,
-                )
-            return bank
+        x_sc = keep.tile([P, S], U8, name="x_sc", align_bytes=64)
+        nc.vector.tensor_copy(x_sc[:], all_scales[:].indirect(offsets[:]))
 
-        gates = []
-        for b in range(BLOCKS):
-            bank = first_layer(w1_c, w1_s, b, "gate")
-            gate = keep.tile([P, TOK, PACK], F32, name="sig%d" % b)
-            nc.scalar.activation(gate[:], bank[:].rearrange("p t n -> p n t"), SIGMOID)
-            gates.append(gate)
+        def deal(copy, grouped, raw, t0):
+            copy(
+                grouped.rearrange("p t m j -> p m j t"),
+                raw.rearrange("p j (m t) -> p m j t", t=PACK)[:, :, :, t0 : t0 + 2],
+            )
 
-        deal(nc.vector.tensor_copy, w3_g[0], w3_raw[0], 0, 4)
-        quantise_half(w3_c, w3_s, w3_g[0], 0)
-        deal(nc.vector.tensor_copy, w3_g[1], w3_raw[1], 0, 4)
-        quantise_half(w3_c, w3_s, w3_g[1], 1)
+        def quantise(codes, scales, values):
+            nc.vector.quantize_mx(out=codes.bitcast(FP8X4), scales=scales, in_=values.rearrange("p m j -> p (m j)"))
 
-        w2_g = keep.tile([P, N, PACK], BF16, name="w2_g", align_bytes=64)
-        w2_c = keep.tile([P, N], U32, name="w2_c", align_bytes=64)
-        w2_s = keep.tile([P, N], U8, name="w2_s", align_bytes=64)
-        nc.scalar.copy(w2_g[:], w2_raw[:].rearrange("p j n -> p n j"))
+        def mx_tiles(name):
+            codes = keep.tile([P, P], U32, name=name + "_codes", align_bytes=64)
+            scales = keep.tile([P, P], U8, name=name + "_scales", align_bytes=64)
+            return codes, scales
 
-        def hidden(b):
-            bank = first_layer(w3_c, w3_s, b, "up")
-            h = keep.tile([P, TOK, PACK], BF16, name="h%d" % b, align_bytes=64)
-            nc.vector.tensor_tensor(h[:], bank[:].rearrange("p t n -> p n t"), gates[b][:], MULT)
-            return h
-
-        def second_layer(h, b):
-            h_c = keep.tile([P, TOK], U32, name="h_c%d" % b, align_bytes=64)
-            h_s = keep.tile([P, TOK], U8, name="h_s%d" % b, align_bytes=64)
-            nc.vector.quantize_mx(out=h_c[:].bitcast(FP8X4), scales=h_s[:], in_=h[:].rearrange("p n t -> p (n t)"))
-            bank = psum.tile([P, TOK], F32, name="y%d" % b, tag="gate")
+        def product(out_ap, weights, moving):
             nc.tensor.matmul_mx(
-                out=bank[:],
-                lhsT=w2_c[:].bitcast(FP8X4),
-                lhsT_scale=w2_s[:],
-                rhs=h_c[:].bitcast(FP8X4),
-                rhs_scale=h_s[:],
+                out=out_ap,
+                lhsT=weights[0].bitcast(FP8X4),
+                lhsT_scale=weights[1],
+                rhs=moving[0].bitcast(FP8X4),
+                rhs_scale=moving[1],
                 start=True,
                 stop=True,
             )
-            y = keep.tile([P, TOK], F32, name="y_sb%d" % b)
+
+        def first_layer(weights, b, bank_tag):
+            bank = psum.tile([P, PACK, TOK], F32, name="first_" + bank_tag, tag=bank_tag)
+            for t in SLOT_ORDER:
+                product(bank[:, t, :], (weights[t][0][:], weights[t][1][:]), (x_w[b][:], x_sc[:, b * TOK : (b + 1) * TOK]))
+            return bank
+
+        def sigmoid(bank, gate):
+            nc.scalar.activation(gate, bank[:].rearrange("p t n -> p n t"), SIGMOID)
+            return gate
+
+        w1_q = [mx_tiles("w1_%d" % t) for t in range(PACK)]
+        w3_q = [mx_tiles("w3_%d" % t) for t in range(PACK)]
+
+        w1_g = [keep.tile([P, 2, P, PACK], BF16, name="w1_g%d" % u, align_bytes=64) for u in range(2)]
+        deal(nc.scalar.copy, w1_g[1][:, :, :HM, :], w1_raw[0][:], 2)
+        deal(nc.scalar.copy, w1_g[0][:, :, :HM, :], w1_raw[0][:], 0)
+        deal(nc.scalar.copy, w1_g[1][:, :, HM:, :], w1_raw[1][:], 2)
+        deal(nc.scalar.copy, w1_g[0][:, :, HM:, :], w1_raw[1][:], 0)
+        for t in SLOT_ORDER:
+            quantise(w1_q[t][0][:], w1_q[t][1][:], w1_g[t // 2][:, t % 2, :, :])
+
+        gate_banks = [first_layer(w1_q, b, "bank%d" % b) for b in range(BLOCKS - 1)]
+
+        for half in range(2):
+            grouped = [
+                keep.tile([P, 2, HM, PACK], BF16, name="w3_g%d%d" % (half, u), tag="w3_g%d%d" % (half, u), align_bytes=64)
+                for u in range(2)
+            ]
+            deal(nc.vector.tensor_copy, grouped[1][:], w3_raw[half][:], 2)
+            m0 = half * HM // 2
+            if m0:
+                deal(nc.vector.tensor_copy, grouped[0][:, :, :m0, :], w3_raw[half][:, :, : PACK * m0], 0)
+            deal(nc.scalar.copy, grouped[0][:, :, m0:, :], w3_raw[half][:, :, PACK * m0 :], 0)
+            cols = slice(half * HM, (half + 1) * HM)
+            for t in SLOT_ORDER:
+                quantise(w3_q[t][0][:, cols], w3_q[t][1][:, cols], grouped[t // 2][:, t % 2, :, :])
+
+        early_gates = keep.tile([P, BLOCKS - 1, TOK, PACK], F32, name="early_gates", tag="w3_raw1")
+        gates = [sigmoid(gate_banks[b], early_gates[:, b, :, :]) for b in range(BLOCKS - 1)]
+
+        up_banks = [first_layer(w3_q, b, "bank%d" % (b + 3)) for b in range(BLOCKS)]
+
+        w2_g = keep.tile([P, N, PACK], BF16, name="w2_g", tag="w3_g10", align_bytes=64)
+        w2_q = mx_tiles("w2")
+        nc.vector.tensor_copy(
+            w2_g[:].rearrange("p (c i) j -> p c j i", i=4),
+            w2_raw[:].rearrange("p j (c i) -> p c j i", i=4),
+        )
+        quantise(w2_q[0][:], w2_q[1][:], w2_g[:])
+
+        def hidden(b):
+            h = keep.tile([P, TOK, PACK], BF16, name="h%d" % b, align_bytes=64)
+            nc.vector.tensor_tensor(h[:], up_banks[b][:].rearrange("p t n -> p n t"), gates[b], MULT)
+            return h
+
+        def quantise_hidden(b):
+            h_q = mx_tiles("h%d" % b)
+            quantise(h_q[0][:], h_q[1][:], hs[b][:])
+            return h_q
+
+        hs = [hidden(0)]
+        last_gate = keep.tile([P, TOK, PACK], F32, name="last_gate")
+        gates.append(sigmoid(first_layer(w1_q, 3, "bank3"), last_gate[:]))
+        hs.append(hidden(1))
+        h_qs = [quantise_hidden(0)]
+        hs.append(hidden(2))
+        h_qs.append(quantise_hidden(1))
+        hs.append(hidden(3))
+        h_qs.append(quantise_hidden(2))
+        h_qs.append(quantise_hidden(3))
+
+        for b in range(BLOCKS):
+            bank = psum.tile([P, TOK], F32, name="second%d" % b, tag="bank%d" % ((0, 1, 2, 7)[b]))
+            product(bank[:], (w2_q[0][:], w2_q[1][:]), (h_qs[b][0][:], h_qs[b][1][:]))
+            y = keep.tile([P, TOK], F32, name="y%d" % b)
             nc.scalar.copy(y[:], bank[:])
             nc.sync.dma_start(out[:, b * TOK : (b + 1) * TOK], y[:])
-
-        hs = [hidden(0), hidden(1)]
-        nc.vector.quantize_mx(out=w2_c[:].bitcast(FP8X4), scales=w2_s[:], in_=w2_g[:].rearrange("p n j -> p (n j)"))
-        for b in range(BLOCKS):
-            second_layer(hs[b], b)
-            if b + 2 < BLOCKS:
-                hs.append(hidden(b + 2))

@@ -149,19 +149,29 @@ def tile_picked_pick_glu_sigmoid_srt_p_kernel(tc, x_words, x_scales, w1, w3, w2,
             quantise(h_q[0][:], h_q[1][:], hs[b][:])
             return h_q
 
-        hs = [hidden(0)]
         last_gate = keep.tile([P, TOK, PACK], F32, name="last_gate")
-        gates.append(sigmoid(first_layer(w1_q, 3, "bank3"), last_gate[:]))
-        hs.append(hidden(1))
+        gates.append(sigmoid(first_layer(w1_q, 3, "bank0"), last_gate[:]))
+        last_up = keep.tile([P, TOK // 2, PACK], F32, name="last_up")
+        nc.scalar.copy(last_up[:], up_banks[3][:, :, TOK // 2 :].rearrange("p t n -> p n t"))
+        last_h = keep.tile([P, TOK, PACK], BF16, name="last_h", align_bytes=64)
+        nc.gpsimd.tensor_tensor(last_h[:, TOK // 2 :, :], last_up[:], last_gate[:, TOK // 2 :, :], MULT)
+
+        hs = [hidden(0), hidden(1)]
         h_qs = [quantise_hidden(0)]
         hs.append(hidden(2))
+        nc.vector.tensor_tensor(
+            last_h[:, : TOK // 2, :],
+            up_banks[3][:, :, : TOK // 2].rearrange("p t n -> p n t"),
+            last_gate[:, : TOK // 2, :],
+            MULT,
+        )
+        hs.append(last_h)
         h_qs.append(quantise_hidden(1))
-        hs.append(hidden(3))
         h_qs.append(quantise_hidden(2))
         h_qs.append(quantise_hidden(3))
 
         for b in range(BLOCKS):
-            bank = psum.tile([P, TOK], F32, name="second%d" % b, tag="bank%d" % ((0, 1, 2, 7)[b]))
+            bank = psum.tile([P, TOK], F32, name="second%d" % b, tag="bank%d" % ((7, 1, 2, 0)[b]))
             product(bank[:], (w2_q[0][:], w2_q[1][:]), (h_qs[b][0][:], h_qs[b][1][:]))
             y = keep.tile([P, TOK], F32, name="y%d" % b)
             nc.scalar.copy(y[:], bank[:])

from contextlib import ExitStack

import concourse.mybir as mybir

K, T, S, H, N = 512, 1024, 512, 512, 128
FLOPS = 2 * S * (2 * K * H + H * N)

F32 = mybir.dt.float32
BF16 = mybir.dt.bfloat16
I32 = mybir.dt.int32
U32 = mybir.dt.uint32
U16 = mybir.dt.uint16
U8 = mybir.dt.uint8
FP8X4 = mybir.dt.float8_e4m3fn_x4
SIGMOID = mybir.ActivationFunctionType.Sigmoid
MULT = mybir.AluOpType.mult

P = 128
PACK = 4
TOK = 128
BLOCKS = S // TOK
HALF = H // 2
HM = HALF // PACK
SLOT_ORDER = (2, 3, 0, 1)


def tile_picked_pick_glu_sigmoid_srt_p_kernel(tc, x_words, x_scales, w1, w3, w2, offs, out):
    nc = tc.nc
    with ExitStack() as ctx:
        keep = ctx.enter_context(tc.tile_pool(name="keep", bufs=1))
        psum = ctx.enter_context(tc.psum_pool(name="psum", bufs=1))

        all_scales = keep.tile([P, T], U8, name="all_scales", align_bytes=64)
        nc.vector.memset(all_scales[:].bitcast(I32), 0)
        warm_in = keep.tile([P, 1], F32, name="warm_in")
        warm_out = keep.tile([P, 1], F32, name="warm_out")
        nc.vector.memset(warm_in[:], 0.0)
        nc.scalar.activation(warm_out[:], warm_in[:], SIGMOID)

        def load_half(w, half, name):
            raw = keep.tile([P, PACK, HALF], F32, name=name, tag=name)
            nc.sync.dma_start(raw[:], w.rearrange("(p j) c -> p j c", j=PACK)[:, :, half * HALF : (half + 1) * HALF])
            return raw

        all_words = keep.tile([P, T], I32, name="all_words", align_bytes=64)
        nc.sync.dma_start(all_words[:], x_words[0].rearrange("p c r -> p (c r)").bitcast(I32))
        offsets = keep.tile([P, S // 16], U16, name="offsets")
        nc.sync.dma_start(offsets[:], offs)
        for r in range(4):
            nc.sync.dma_start(all_scales[r:P:32, :].bitcast(I32), x_scales[0, r:16:4, :].bitcast(I32))
        w1_raw = [load_half(w1, half, "w1_raw%d" % half) for half in range(2)]
        w3_raw = [load_half(w3, half, "w3_raw%d" % half) for half in range(2)]
        w2_raw = keep.tile([P, PACK, N], F32, name="w2_raw")
        nc.sync.dma_start(w2_raw[:], w2.rearrange("(p j) n -> p j n", j=PACK))

        x_w = []
        for b in range(BLOCKS):
            words = keep.tile([P, TOK], U32, name="x_w%d" % b, align_bytes=64)
            nc.vector.tensor_copy(
                words[:], all_words[:].bitcast(U32).indirect(offsets[:, b * (TOK // 16) : (b + 1) * (TOK // 16)])
            )
            x_w.append(words)

        x_sc = keep.tile([P, S], U8, name="x_sc", align_bytes=64)
        nc.vector.tensor_copy(x_sc[:], all_scales[:].indirect(offsets[:]))

        def deal(copy, grouped, raw, t0):
            copy(
                grouped.rearrange("p t m j -> p m j t"),
                raw.rearrange("p j (m t) -> p m j t", t=PACK)[:, :, :, t0 : t0 + 2],
            )

        def quantise(codes, scales, values):
            nc.vector.quantize_mx(out=codes.bitcast(FP8X4), scales=scales, in_=values.rearrange("p m j -> p (m j)"))

        def mx_tiles(name):
            codes = keep.tile([P, P], U32, name=name + "_codes", align_bytes=64)
            scales = keep.tile([P, P], U8, name=name + "_scales", align_bytes=64)
            return codes, scales

        def product(out_ap, weights, moving):
            nc.tensor.matmul_mx(
                out=out_ap,
                lhsT=weights[0].bitcast(FP8X4),
                lhsT_scale=weights[1],
                rhs=moving[0].bitcast(FP8X4),
                rhs_scale=moving[1],
                start=True,
                stop=True,
            )

        def first_layer(weights, b, bank_tag):
            bank = psum.tile([P, PACK, TOK], F32, name="first_" + bank_tag, tag=bank_tag)
            for t in SLOT_ORDER:
                product(bank[:, t, :], (weights[t][0][:], weights[t][1][:]), (x_w[b][:], x_sc[:, b * TOK : (b + 1) * TOK]))
            return bank

        def sigmoid(bank, gate):
            nc.scalar.activation(gate, bank[:].rearrange("p t n -> p n t"), SIGMOID)
            return gate

        w1_q = [mx_tiles("w1_%d" % t) for t in range(PACK)]
        w3_q = [mx_tiles("w3_%d" % t) for t in range(PACK)]

        w1_g = [keep.tile([P, 2, P, PACK], BF16, name="w1_g%d" % u, align_bytes=64) for u in range(2)]
        deal(nc.scalar.copy, w1_g[1][:, :, :HM, :], w1_raw[0][:], 2)
        deal(nc.scalar.copy, w1_g[0][:, :, :HM, :], w1_raw[0][:], 0)
        deal(nc.scalar.copy, w1_g[1][:, :, HM:, :], w1_raw[1][:], 2)
        deal(nc.scalar.copy, w1_g[0][:, :, HM:, :], w1_raw[1][:], 0)
        for t in SLOT_ORDER:
            quantise(w1_q[t][0][:], w1_q[t][1][:], w1_g[t // 2][:, t % 2, :, :])

        gate_banks = [first_layer(w1_q, b, "bank%d" % b) for b in range(BLOCKS - 1)]

        for half in range(2):
            grouped = [
                keep.tile([P, 2, HM, PACK], BF16, name="w3_g%d%d" % (half, u), tag="w3_g%d%d" % (half, u), align_bytes=64)
                for u in range(2)
            ]
            deal(nc.vector.tensor_copy, grouped[1][:], w3_raw[half][:], 2)
            m0 = half * HM // 2
            if m0:
                deal(nc.vector.tensor_copy, grouped[0][:, :, :m0, :], w3_raw[half][:, :, : PACK * m0], 0)
            deal(nc.scalar.copy, grouped[0][:, :, m0:, :], w3_raw[half][:, :, PACK * m0 :], 0)
            cols = slice(half * HM, (half + 1) * HM)
            for t in SLOT_ORDER:
                quantise(w3_q[t][0][:, cols], w3_q[t][1][:, cols], grouped[t // 2][:, t % 2, :, :])

        early_gates = keep.tile([P, BLOCKS - 1, TOK, PACK], F32, name="early_gates", tag="w3_raw1")
        gates = [sigmoid(gate_banks[b], early_gates[:, b, :, :]) for b in range(BLOCKS - 1)]

        up_banks = [first_layer(w3_q, b, "bank%d" % (b + 3)) for b in range(BLOCKS)]

        w2_g = keep.tile([P, N, PACK], BF16, name="w2_g", tag="w3_g10", align_bytes=64)
        w2_q = mx_tiles("w2")
        nc.vector.tensor_copy(
            w2_g[:].rearrange("p (c i) j -> p c j i", i=4),
            w2_raw[:].rearrange("p j (c i) -> p c j i", i=4),
        )
        quantise(w2_q[0][:], w2_q[1][:], w2_g[:])

        def hidden(b):
            h = keep.tile([P, TOK, PACK], BF16, name="h%d" % b, align_bytes=64)
            nc.vector.tensor_tensor(h[:], up_banks[b][:].rearrange("p t n -> p n t"), gates[b], MULT)
            return h

        def quantise_hidden(b):
            h_q = mx_tiles("h%d" % b)
            quantise(h_q[0][:], h_q[1][:], hs[b][:])
            return h_q

        last_gate = keep.tile([P, TOK, PACK], F32, name="last_gate")
        gates.append(sigmoid(first_layer(w1_q, 3, "bank0"), last_gate[:]))
        last_up = keep.tile([P, TOK // 2, PACK], F32, name="last_up")
        nc.scalar.copy(last_up[:], up_banks[3][:, :, TOK // 2 :].rearrange("p t n -> p n t"))
        last_h = keep.tile([P, TOK, PACK], BF16, name="last_h", align_bytes=64)
        nc.gpsimd.tensor_tensor(last_h[:, TOK // 2 :, :], last_up[:], last_gate[:, TOK // 2 :, :], MULT)

        hs = [hidden(0), hidden(1)]
        h_qs = [quantise_hidden(0)]
        hs.append(hidden(2))
        nc.vector.tensor_tensor(
            last_h[:, : TOK // 2, :],
            up_banks[3][:, :, : TOK // 2].rearrange("p t n -> p n t"),
            last_gate[:, : TOK // 2, :],
            MULT,
        )
        hs.append(last_h)
        h_qs.append(quantise_hidden(1))
        h_qs.append(quantise_hidden(2))
        h_qs.append(quantise_hidden(3))

        for b in range(BLOCKS):
            bank = psum.tile([P, TOK], F32, name="second%d" % b, tag="bank%d" % ((7, 1, 2, 0)[b]))
            product(bank[:], (w2_q[0][:], w2_q[1][:]), (h_qs[b][0][:], h_qs[b][1][:]))
            y = keep.tile([P, TOK], F32, name="y%d" % b)
            nc.scalar.copy(y[:], bank[:])
            nc.sync.dma_start(out[:, b * TOK : (b + 1) * TOK], y[:])
